import numpy as np
import ml_dtypes


def mxq(x, axis, fmt="e4m3"):
    dtype, down = {"e4m3": (ml_dtypes.float8_e4m3fn, 7), "e5m2": (ml_dtypes.float8_e5m2, 14)}[fmt]
    v = np.moveaxis(np.asarray(x, np.float32).astype(ml_dtypes.bfloat16).astype(np.float64), axis, -1)
    blocks = v.reshape(v.shape[:-1] + (-1, 32))
    amax = np.abs(blocks).max(-1, keepdims=True)
    byte = np.maximum(np.where(amax > 0, np.frexp(amax)[1] - 1 + 127, 0) - down, 1)
    scale = np.exp2(byte - 127.0)
    codes = (blocks / scale).astype(np.float32).astype(dtype).astype(np.float64)
    return np.moveaxis((codes * scale).reshape(v.shape), -1, axis)


WIDE = False


def mx_kscale(k):
    if not WIDE:
        return np.ones(k)
    levels = np.array([10, -10, 5, -5, 0])
    if k % 512:
        return np.exp2(np.random.permutation(np.resize(levels, k // 32))).repeat(32)
    a = np.empty((k // 512, 16))
    for p in range(k // 512):
        a[p, :8] = np.random.permutation(np.resize(levels, 8))
        for g in range(8):
            far = levels[np.abs(levels - a[p, g]) >= 10]
            a[p, g + 8] = far[np.random.randint(len(far))]
    return np.exp2(a.ravel()).repeat(32)


def f64(x):
    return np.asarray(x).astype(np.float64)


def striped(idx):
    return np.tile(idx.reshape(-1, 16).T, (8, 1)).astype(np.uint16)


def unstriped(offs):
    return offs[:16].T.reshape(-1).astype(np.int64)


def pack_weight(w):
    k, n = w.shape
    w = f64(np.asarray(w, np.float32).astype(ml_dtypes.bfloat16)).reshape(k // 32, 32, n)
    amax = np.abs(w).max(1)
    byte = np.clip(np.where(amax > 0, np.frexp(amax)[1] - 1 + 127 - 7, 1), 1, 254)
    scaled = (w * np.exp2(127.0 - byte)[:, None, :]).reshape(k, n).astype(np.float32)
    words = np.ascontiguousarray(scaled.reshape(k // 512, 128, 4, n).transpose(0, 1, 3, 2)).astype(ml_dtypes.float8_e4m3fn).view(np.uint8)
    return words, np.ascontiguousarray(byte.astype(np.uint8).reshape(k // 512, 16, n))


def unpack_weight(words, scales):
    g, p, n, _ = words.shape
    vals = np.ascontiguousarray(words).view(ml_dtypes.float8_e4m3fn).astype(np.float64) * np.repeat(np.exp2(scales.astype(np.float64) - 127.0), 8, axis=1)[..., None]
    return vals.transpose(0, 1, 3, 2).reshape(g * 512, n)


K, T, S, N, U = 1024, 1024, 512, 128, 1024
P = 2 ** 7


def setup_inputs():
    n = np.random.standard_normal
    s = mx_kscale(K)[:, None]
    packed_w1 = pack_weight(n((K, N)) / np.sqrt(K) / s)
    return {
        "xT": (n((K, T)) * s).astype(np.float32),
        "mem": n((N, U)).astype(np.float32),
        "w1_words": packed_w1[0],
        "w1_scales": packed_w1[1],
        "old": np.tile(np.random.uniform(0.5, 0.95, S), (P, 1)).astype(np.float32),
        "new": np.tile(np.random.uniform(0.05, 0.5, S), (P, 1)).astype(np.float32),
        "offs": striped(np.random.permutation(T)[:S]),
        "slot": striped(np.random.permutation(U)[:S]),
    }


def reference(xT, mem, w1_words, w1_scales, old, new, offs, slot):
    xq = mxq(f64(xT)[:, unstriped(offs)], 0, "e4m3")
    y = unpack_weight(w1_words, w1_scales).T @ xq
    out = f64(mem).copy()
    out[:, unstriped(slot)] = f64(mem)[:, unstriped(slot)] * f64(old)[:1] + y * f64(new)[:1]
    return out

@@ -1,0 +1,146 @@
+from contextlib import ExitStack
+
+import concourse.mybir as mybir
+from concourse.masks import make_identity
+
+K, T, S, N, U = 1024, 1024, 512, 128, 1024
+FLOPS = 2 * K * N * S
+
+F32 = mybir.dt.float32
+BF16 = mybir.dt.bfloat16
+I32 = mybir.dt.int32
+U32 = mybir.dt.uint32
+U16 = mybir.dt.uint16
+U8 = mybir.dt.uint8
+FP8X4 = mybir.dt.float8_e4m3fn_x4
+MULT = mybir.AluOpType.mult
+ADD = mybir.AluOpType.add
+
+P = 128
+CH = 128
+NCH = S // CH
+LC = CH // 16
+
+PIECES = (
+    ((0, 512, 512), (512, 512, 192)),
+    ((0, 512, 512), (512, 512, 192)),
+    ((0, 512, 512), (512, 512, 192)),
+    ((0, 512, 512), (512, 256, 0), (768, 256, 128)),
+)
+
+
+def tile_picked_ema_none_e_kernel(tc, xT, mem, w1_words, w1_scales, old, new, offs, slot, out):
+    nc = tc.nc
+    with ExitStack() as ctx:
+        keep = ctx.enter_context(tc.tile_pool(name="keep", bufs=1))
+        psum = ctx.enter_context(tc.psum_pool(name="psum", bufs=1))
+
+        x_rows = xT.rearrange("(z p u e) t -> z u p e t", z=2, p=P, u=2, e=2)
+
+        offs_sb = keep.tile([P, S // 16], U16, name="offs_sb")
+        slot_sb = keep.tile([P, S // 16], U16, name="slot_sb")
+        mem_sb = keep.tile([P, U], F32, name="mem_sb")
+        old_col = keep.tile([P, 4], F32, name="old_col")
+        new_sb = keep.tile([P, S], F32, name="new_sb")
+        w_words = keep.tile([P, 2, N], U32, name="w_words", align_bytes=64)
+        w_scales = keep.tile([P, 2, N], U8, name="w_scales", align_bytes=64)
+        ident = keep.tile([P, P], F32, name="ident")
+
+        raw = {}
+        for pair in range(4):
+            for c0, width, by_scalar in PIECES[pair]:
+                raw[pair, c0] = keep.tile([P, 2, width], F32, name="raw_%d_%d" % (pair, c0))
+
+        def load_x(pair, c0, width):
+            nc.sync.dma_start(out=raw[pair, c0][:], in_=x_rows[pair // 2, pair % 2, :, :, c0 : c0 + width])
+
+        nc.sync.dma_start(out=mem_sb[:], in_=mem)
+        nc.scalar.dma_start(out=old_col[:], in_=old[0, :].rearrange("(p c) -> p c", c=4))
+        nc.sync.dma_start(slot_sb[:], slot)
+        load_x(0, 0, 512)
+        nc.sync.dma_start(offs_sb[:], offs)
+        for pair in range(4):
+            for c0, width, by_scalar in PIECES[pair]:
+                if (pair, c0) != (0, 0):
+                    load_x(pair, c0, width)
+        nc.sync.dma_start(out=w_words[:].bitcast(I32), in_=w1_words.rearrange("z p n r -> p z (n r)").bitcast(I32))
+        nc.sync.dma_start(out=new_sb[:], in_=new)
+
+        make_identity(nc, ident[:])
+        nc.gpsimd.memset(w_scales[:], 0)
+        scale_rows = w1_scales.rearrange("z (q r) c -> r q z c", r=4)
+        for r in range(4):
+            nc.gpsimd.dma_start(out=w_scales[r:P:32, :, :].bitcast(I32), in_=scale_rows[r].bitcast(I32))
+
+        old_ps = psum.tile([P, 4, P], F32, name="old_ps")
+        for c in range(4):
+            nc.tensor.transpose(old_ps[:, c, :], old_col[:, c : c + 1].to_broadcast([P, P]), ident[:])
+
+        picked_mem = keep.tile([P, S], F32, name="picked_mem", tag="turns", align_bytes=64)
+        kept = keep.tile([P, S], F32, name="kept")
+        nc.vector.tensor_copy(picked_mem[:], mem_sb[:].indirect(slot_sb[:]))
+        nc.vector.tensor_tensor(
+            kept[:].rearrange("p (n c) -> p n c", c=4),
+            picked_mem[:].rearrange("p (n c) -> p n c", c=4),
+            old_ps[:].rearrange("p c n -> p n c"),
+            MULT,
+        )
+
+        starts = [704 + 704 + 512, 704 + 512, 512, 0]
+        chain = keep.tile([P, 2 * (T + starts[0])], BF16, name="chain")
+        pairs = [chain[:, 2 * s : 2 * (s + T)] for s in starts]
+
+        def cast(pair):
+            dst = pairs[pair].rearrange("p (t e) -> p t e", e=2)
+            for c0, width, by_scalar in PIECES[pair]:
+                src = raw[pair, c0][:].rearrange("p e t -> p t e")
+                if by_scalar > 0:
+                    nc.scalar.copy(dst[:, c0 : c0 + by_scalar, :], src[:, 0:by_scalar, :])
+                if by_scalar < width:
+                    nc.vector.tensor_copy(dst[:, c0 + by_scalar : c0 + width, :], src[:, by_scalar:width, :])
+
+        quad0 = keep.tile([P, 4 * S], BF16, name="quad0", tag="turns", align_bytes=64)
+        codes0 = keep.tile([P, S], U32, name="codes0", align_bytes=64)
+        scales0 = keep.tile([P, S], U8, name="scales0", align_bytes=64)
+        quad0_words = quad0[:].bitcast(U32).rearrange("p (n u) -> p n u", u=2)
+        for u in range(2):
+            cast(u)
+            nc.vector.tensor_copy(quad0_words[:, :, u], pairs[u].bitcast(U32).indirect(offs_sb[:]))
+        nc.vector.quantize_mx(out=codes0[:].bitcast(FP8X4), scales=scales0[:], in_=quad0[:])
+
+        halves = keep.tile([P, 2 * S], U32, name="halves")
+        quad1 = [keep.tile([P, 4 * CH], BF16, name="quad1_%d" % c, align_bytes=64) for c in range(NCH)]
+        codes1 = [keep.tile([P, CH], U32, name="codes1_%d" % c, align_bytes=64) for c in range(NCH)]
+        scales1 = [keep.tile([P, CH], U8, name="scales1_%d" % c, align_bytes=64) for c in range(NCH)]
+        y_ps = [psum.tile([P, CH], F32, name="y_ps_%d" % c) for c in range(NCH)]
+        moved = keep.tile([P, S], F32, name="moved")
+        cast(2)
+        nc.vector.tensor_copy(halves[:].rearrange("p (c u n) -> p c u n", u=2, n=CH)[:, :, 0, :], pairs[2].bitcast(U32).indirect(offs_sb[:]))
+        cast(3)
+        for c in range(NCH):
+            nc.vector.tensor_copy(halves[:, (2 * c + 1) * CH : (2 * c + 2) * CH], pairs[3].bitcast(U32).indirect(offs_sb[:, c * LC : (c + 1) * LC]))
+        for c in range(NCH):
+            cols = slice(c * CH, (c + 1) * CH)
+            nc.tensor.matmul_mx(out=y_ps[c][:], lhsT=w_words[:, 0, :].bitcast(FP8X4), lhsT_scale=w_scales[:, 0, :],
+                                rhs=codes0[:, cols].bitcast(FP8X4), rhs_scale=scales0[:, cols], start=True, stop=False)
+        for c in range(NCH):
+            nc.scalar.copy(quad1[c][:].bitcast(U32).rearrange("p (n u) -> p n u", u=2), halves[:, 2 * c * CH : (2 * c + 2) * CH].rearrange("p (u n) -> p n u", u=2))
+            nc.vector.quantize_mx(out=codes1[c][:].bitcast(FP8X4), scales=scales1[c][:], in_=quad1[c][:])
+            nc.tensor.matmul_mx(out=y_ps[c][:], lhsT=w_words[:, 1, :].bitcast(FP8X4), lhsT_scale=w_scales[:, 1, :],
+                                rhs=codes1[c][:].bitcast(FP8X4), rhs_scale=scales1[c][:], start=False, stop=True)
+
+        def weigh(c):
+            cols = slice(c * CH, (c + 1) * CH)
+            nc.vector.tensor_tensor(moved[:, cols], y_ps[c][:], new_sb[:, cols], MULT)
+
+        def put(c0, c1):
+            cols = slice(c0 * CH, c1 * CH)
+            nc.vector.tensor_tensor(mem_sb[:].indirect(slot_sb[:, c0 * LC : c1 * LC]), moved[:, cols], kept[:, cols], ADD)
+
+        weigh(0)
+        weigh(1)
+        put(0, 1)
+        weigh(2)
+        weigh(3)
+        put(1, NCH)
+        nc.sync.dma_start(out=out, in_=mem_sb[:])

@@ -22,10 +22,10 @@ NCH = S // CH
 LC = CH // 16
 
 PIECES = (
-    ((0, 512, 512), (512, 512, 192)),
-    ((0, 512, 512), (512, 512, 192)),
-    ((0, 512, 512), (512, 512, 192)),
-    ((0, 512, 512), (512, 256, 0), (768, 256, 128)),
+    ((0, 1024, 384),),
+    ((0, 1024, 512),),
+    ((0, 512, 512), (512, 512, 512)),
+    ((0, 512, 512), (512, 512, 256)),
 )
 
 
@@ -49,46 +49,44 @@ def tile_picked_ema_none_e_kernel(tc, xT, mem, w1_words, w1_scales, old, new, of
         raw = {}
         for pair in range(4):
             for c0, width, by_scalar in PIECES[pair]:
-                raw[pair, c0] = keep.tile([P, 2, width], F32, name="raw_%d_%d" % (pair, c0))
+                raw[pair, c0] = keep.tile([P, 2, width], F32, name="raw_%d_%d" % (pair, c0), tag="raw_%d_%d" % (pair, c0), align_bytes=64)
 
         def load_x(pair, c0, width):
             nc.sync.dma_start(out=raw[pair, c0][:], in_=x_rows[pair // 2, pair % 2, :, :, c0 : c0 + width])
 
-        nc.sync.dma_start(out=mem_sb[:], in_=mem)
-        nc.scalar.dma_start(out=old_col[:], in_=old[0, :].rearrange("(p c) -> p c", c=4))
-        nc.sync.dma_start(slot_sb[:], slot)
-        load_x(0, 0, 512)
-        nc.sync.dma_start(offs_sb[:], offs)
-        for pair in range(4):
-            for c0, width, by_scalar in PIECES[pair]:
-                if (pair, c0) != (0, 0):
-                    load_x(pair, c0, width)
-        nc.sync.dma_start(out=w_words[:].bitcast(I32), in_=w1_words.rearrange("z p n r -> p z (n r)").bitcast(I32))
-        nc.sync.dma_start(out=new_sb[:], in_=new)
-
         make_identity(nc, ident[:])
+        nc.sync.dma_start(out=old_col[:], in_=old[0, :].rearrange("(p c) -> p c", c=4))
+        nc.sync.dma_start(out=mem_sb[:], in_=mem)
+        nc.sync.dma_start(slot_sb[:], slot)
+        load_x(0, 0, 1024)
+        nc.sync.dma_start(offs_sb[:], offs)
+        load_x(1, 0, 1024)
+        load_x(2, 0, 512)
         nc.gpsimd.memset(w_scales[:], 0)
         scale_rows = w1_scales.rearrange("z (q r) c -> r q z c", r=4)
         for r in range(4):
-            nc.gpsimd.dma_start(out=w_scales[r:P:32, :, :].bitcast(I32), in_=scale_rows[r].bitcast(I32))
+            nc.sync.dma_start(out=w_scales[r:P:32, :, :].bitcast(I32), in_=scale_rows[r].bitcast(I32))
+        load_x(2, 512, 512)
+        load_x(3, 0, 512)
+        load_x(3, 512, 512)
+        nc.sync.dma_start(out=w_words[:].bitcast(I32), in_=w1_words.rearrange("z p n r -> p z (n r)").bitcast(I32))
+        nc.sync.dma_start(out=new_sb[:], in_=new)
+
 
         old_ps = psum.tile([P, 4, P], F32, name="old_ps")
         for c in range(4):
             nc.tensor.transpose(old_ps[:, c, :], old_col[:, c : c + 1].to_broadcast([P, P]), ident[:])
 
+        old_sb = keep.tile([P, S], F32, name="old_sb")
+        nc.scalar.copy(old_sb[:].rearrange("p (n c) -> p n c", c=4), old_ps[:].rearrange("p c n -> p n c"))
         picked_mem = keep.tile([P, S], F32, name="picked_mem", tag="turns", align_bytes=64)
         kept = keep.tile([P, S], F32, name="kept")
         nc.vector.tensor_copy(picked_mem[:], mem_sb[:].indirect(slot_sb[:]))
-        nc.vector.tensor_tensor(
-            kept[:].rearrange("p (n c) -> p n c", c=4),
-            picked_mem[:].rearrange("p (n c) -> p n c", c=4),
-            old_ps[:].rearrange("p c n -> p n c"),
-            MULT,
-        )
+        nc.vector.tensor_tensor(kept[:], picked_mem[:], old_sb[:], MULT)
 
-        starts = [704 + 704 + 512, 704 + 512, 512, 0]
-        chain = keep.tile([P, 2 * (T + starts[0])], BF16, name="chain")
-        pairs = [chain[:, 2 * s : 2 * (s + T)] for s in starts]
+        homes = ["turns", "raw_0_0", "raw_1_0", "raw_2_512"]
+        pair_tiles = [keep.tile([P, 2 * T], BF16, name="pairs_%d" % i, tag=homes[i], align_bytes=64) for i in range(4)]
+        pairs = [t[:] for t in pair_tiles]
 
         def cast(pair):
             dst = pairs[pair].rearrange("p (t e) -> p t e", e=2)
@@ -99,14 +97,21 @@ def tile_picked_ema_none_e_kernel(tc, xT, mem, w1_words, w1_scales, old, new, of
                 if by_scalar < width:
                     nc.vector.tensor_copy(dst[:, c0 + by_scalar : c0 + width, :], src[:, by_scalar:width, :])
 
-        quad0 = keep.tile([P, 4 * S], BF16, name="quad0", tag="turns", align_bytes=64)
+        H = S // 2
+        halves0 = keep.tile([P, 2 * S], U32, name="halves0")
+        quad0 = keep.tile([P, 4 * S], BF16, name="quad0", align_bytes=64)
         codes0 = keep.tile([P, S], U32, name="codes0", align_bytes=64)
         scales0 = keep.tile([P, S], U8, name="scales0", align_bytes=64)
-        quad0_words = quad0[:].bitcast(U32).rearrange("p (n u) -> p n u", u=2)
-        for u in range(2):
-            cast(u)
-            nc.vector.tensor_copy(quad0_words[:, :, u], pairs[u].bitcast(U32).indirect(offs_sb[:]))
-        nc.vector.quantize_mx(out=codes0[:].bitcast(FP8X4), scales=scales0[:], in_=quad0[:])
+        cast(0)
+        nc.vector.tensor_copy(halves0[:].rearrange("p (h u n) -> p h u n", u=2, n=H)[:, :, 0, :], pairs[0].bitcast(U32).indirect(offs_sb[:]))
+        cast(1)
+        for h in range(2):
+            nc.vector.tensor_copy(halves0[:, (2 * h + 1) * H : (2 * h + 2) * H], pairs[1].bitcast(U32).indirect(offs_sb[:, h * H // 16 : (h + 1) * H // 16]))
+        for h in range(2):
+            nc.vector.tensor_copy(quad0[:, 4 * h * H : 4 * (h + 1) * H].bitcast(U32).rearrange("p (n u) -> p n u", u=2),
+                                  halves0[:, 2 * h * H : 2 * (h + 1) * H].rearrange("p (u n) -> p n u", u=2))
+        for h in range(2):
+            nc.vector.quantize_mx(out=codes0[:, h * H : (h + 1) * H].bitcast(FP8X4), scales=scales0[:, h * H : (h + 1) * H], in_=quad0[:, 4 * h * H : 4 * (h + 1) * H])
 
         halves = keep.tile([P, 2 * S], U32, name="halves")
         quad1 = [keep.tile([P, 4 * CH], BF16, name="quad1_%d" % c, align_bytes=64) for c in range(NCH)]

@@ -17,15 +17,16 @@ MULT = mybir.AluOpType.mult
 ADD = mybir.AluOpType.add
 
 P = 128
-CH = 128
-NCH = S // CH
-LC = CH // 16
+PER_COLUMN = 16
+HALF = S // 2
+CHUNK = 128
+CHUNKS = S // CHUNK
 
 PIECES = (
     ((0, 1024, 384),),
     ((0, 1024, 512),),
     ((0, 512, 512), (512, 512, 512)),
-    ((0, 512, 512), (512, 512, 256)),
+    ((0, 512, 512), (512, 512, 288)),
 )
 
 
@@ -35,10 +36,11 @@ def tile_picked_ema_none_e_kernel(tc, xT, mem, w1_words, w1_scales, old, new, of
         keep = ctx.enter_context(tc.tile_pool(name="keep", bufs=1))
         psum = ctx.enter_context(tc.psum_pool(name="psum", bufs=1))
 
-        x_rows = xT.rearrange("(z p u e) t -> z u p e t", z=2, p=P, u=2, e=2)
+        def entries(list_sb, first, last):
+            return list_sb[:, first // PER_COLUMN : last // PER_COLUMN]
 
-        offs_sb = keep.tile([P, S // 16], U16, name="offs_sb")
-        slot_sb = keep.tile([P, S // 16], U16, name="slot_sb")
+        offs_sb = keep.tile([P, S // PER_COLUMN], U16, name="offs_sb")
+        slot_sb = keep.tile([P, S // PER_COLUMN], U16, name="slot_sb")
         mem_sb = keep.tile([P, U], F32, name="mem_sb")
         old_col = keep.tile([P, 4], F32, name="old_col")
         new_sb = keep.tile([P, S], F32, name="new_sb")
@@ -48,104 +50,129 @@ def tile_picked_ema_none_e_kernel(tc, xT, mem, w1_words, w1_scales, old, new, of
 
         raw = {}
         for pair in range(4):
-            for c0, width, by_scalar in PIECES[pair]:
-                raw[pair, c0] = keep.tile([P, 2, width], F32, name="raw_%d_%d" % (pair, c0), tag="raw_%d_%d" % (pair, c0), align_bytes=64)
+            for first, width, by_scalar in PIECES[pair]:
+                label = "raw_%d_%d" % (pair, first)
+                raw[pair, first] = keep.tile([P, 2, width], F32, name=label, tag=label, align_bytes=64)
 
-        def load_x(pair, c0, width):
-            nc.sync.dma_start(out=raw[pair, c0][:], in_=x_rows[pair // 2, pair % 2, :, :, c0 : c0 + width])
+        x_rows = xT.rearrange("(z p u e) t -> z u p e t", z=2, p=P, u=2, e=2)
+
+        def load_x(pair, piece):
+            first, width, by_scalar = PIECES[pair][piece]
+            nc.sync.dma_start(out=raw[pair, first][:], in_=x_rows[pair // 2, pair % 2, :, :, first : first + width])
 
         make_identity(nc, ident[:])
         nc.sync.dma_start(out=old_col[:], in_=old[0, :].rearrange("(p c) -> p c", c=4))
         nc.sync.dma_start(out=mem_sb[:], in_=mem)
         nc.sync.dma_start(slot_sb[:], slot)
-        load_x(0, 0, 1024)
+        load_x(0, 0)
         nc.sync.dma_start(offs_sb[:], offs)
-        load_x(1, 0, 1024)
-        load_x(2, 0, 512)
+        load_x(1, 0)
+        load_x(2, 0)
         nc.gpsimd.memset(w_scales[:], 0)
         scale_rows = w1_scales.rearrange("z (q r) c -> r q z c", r=4)
         for r in range(4):
             nc.sync.dma_start(out=w_scales[r:P:32, :, :].bitcast(I32), in_=scale_rows[r].bitcast(I32))
-        load_x(2, 512, 512)
-        load_x(3, 0, 512)
-        load_x(3, 512, 512)
+        load_x(2, 1)
+        load_x(3, 0)
+        load_x(3, 1)
         nc.sync.dma_start(out=w_words[:].bitcast(I32), in_=w1_words.rearrange("z p n r -> p z (n r)").bitcast(I32))
         nc.sync.dma_start(out=new_sb[:], in_=new)
-
 
         old_ps = psum.tile([P, 4, P], F32, name="old_ps")
         for c in range(4):
             nc.tensor.transpose(old_ps[:, c, :], old_col[:, c : c + 1].to_broadcast([P, P]), ident[:])
-
         old_sb = keep.tile([P, S], F32, name="old_sb")
         nc.scalar.copy(old_sb[:].rearrange("p (n c) -> p n c", c=4), old_ps[:].rearrange("p c n -> p n c"))
-        picked_mem = keep.tile([P, S], F32, name="picked_mem", tag="turns", align_bytes=64)
+
+        picked_mem = keep.tile([P, S], F32, name="picked_mem", tag="picked_mem", align_bytes=64)
         kept = keep.tile([P, S], F32, name="kept")
         nc.vector.tensor_copy(picked_mem[:], mem_sb[:].indirect(slot_sb[:]))
         nc.vector.tensor_tensor(kept[:], picked_mem[:], old_sb[:], MULT)
 
-        homes = ["turns", "raw_0_0", "raw_1_0", "raw_2_512"]
-        pair_tiles = [keep.tile([P, 2 * T], BF16, name="pairs_%d" % i, tag=homes[i], align_bytes=64) for i in range(4)]
-        pairs = [t[:] for t in pair_tiles]
+        window_0 = keep.tile([P, 2 * T], BF16, name="window_0", tag="picked_mem", align_bytes=64)
+        windows_1_2 = keep.tile([P, 4 * T], BF16, name="windows_1_2", tag="raw_0_0", align_bytes=64)
+        window_3 = keep.tile([P, 2 * T], BF16, name="window_3", tag="raw_2_0", align_bytes=64)
+        windows = [window_0[:], windows_1_2[:, 0 : 2 * T], windows_1_2[:, 2 * T : 4 * T], window_3[:]]
 
-        def cast(pair):
-            dst = pairs[pair].rearrange("p (t e) -> p t e", e=2)
-            for c0, width, by_scalar in PIECES[pair]:
-                src = raw[pair, c0][:].rearrange("p e t -> p t e")
-                if by_scalar > 0:
-                    nc.scalar.copy(dst[:, c0 : c0 + by_scalar, :], src[:, 0:by_scalar, :])
+        def round_pair(pair):
+            dst = windows[pair].rearrange("p (t e) -> p t e", e=2)
+            for first, width, by_scalar in PIECES[pair]:
+                src = raw[pair, first][:].rearrange("p e t -> p t e")
+                nc.scalar.copy(dst[:, first : first + by_scalar, :], src[:, 0:by_scalar, :])
                 if by_scalar < width:
-                    nc.vector.tensor_copy(dst[:, c0 + by_scalar : c0 + width, :], src[:, by_scalar:width, :])
+                    nc.vector.tensor_copy(dst[:, first + by_scalar : first + width, :], src[:, by_scalar:width, :])
 
-        H = S // 2
-        halves0 = keep.tile([P, 2 * S], U32, name="halves0")
-        quad0 = keep.tile([P, 4 * S], BF16, name="quad0", align_bytes=64)
-        codes0 = keep.tile([P, S], U32, name="codes0", align_bytes=64)
-        scales0 = keep.tile([P, S], U8, name="scales0", align_bytes=64)
-        cast(0)
-        nc.vector.tensor_copy(halves0[:].rearrange("p (h u n) -> p h u n", u=2, n=H)[:, :, 0, :], pairs[0].bitcast(U32).indirect(offs_sb[:]))
-        cast(1)
-        for h in range(2):
-            nc.vector.tensor_copy(halves0[:, (2 * h + 1) * H : (2 * h + 2) * H], pairs[1].bitcast(U32).indirect(offs_sb[:, h * H // 16 : (h + 1) * H // 16]))
-        for h in range(2):
-            nc.vector.tensor_copy(quad0[:, 4 * h * H : 4 * (h + 1) * H].bitcast(U32).rearrange("p (n u) -> p n u", u=2),
-                                  halves0[:, 2 * h * H : 2 * (h + 1) * H].rearrange("p (u n) -> p n u", u=2))
-        for h in range(2):
-            nc.vector.quantize_mx(out=codes0[:, h * H : (h + 1) * H].bitcast(FP8X4), scales=scales0[:, h * H : (h + 1) * H], in_=quad0[:, 4 * h * H : 4 * (h + 1) * H])
+        def gather_pair(dst, pair, first, last):
+            nc.vector.tensor_copy(dst, windows[pair].bitcast(U32).indirect(entries(offs_sb, first, last)))
 
-        halves = keep.tile([P, 2 * S], U32, name="halves")
-        quad1 = [keep.tile([P, 4 * CH], BF16, name="quad1_%d" % c, align_bytes=64) for c in range(NCH)]
-        codes1 = [keep.tile([P, CH], U32, name="codes1_%d" % c, align_bytes=64) for c in range(NCH)]
-        scales1 = [keep.tile([P, CH], U8, name="scales1_%d" % c, align_bytes=64) for c in range(NCH)]
-        y_ps = [psum.tile([P, CH], F32, name="y_ps_%d" % c) for c in range(NCH)]
+        def as_words(woven):
+            return woven.bitcast(U32).rearrange("p (n u) -> p n u", u=2)
+
+        picked_0 = keep.tile([P, 2 * S], U32, name="picked_0")
+        woven_0 = keep.tile([P, 4 * S], BF16, name="woven_0", align_bytes=64)
+        codes_0_first = keep.tile([P, HALF], U32, name="codes_0_first", align_bytes=64)
+        scales_0 = keep.tile([P, S], U8, name="scales_0", align_bytes=64)
+        round_pair(0)
+        gather_pair(picked_0[:].rearrange("p (h u n) -> p h u n", u=2, n=HALF)[:, :, 0, :], 0, 0, S)
+        round_pair(1)
+        for h in range(2):
+            gather_pair(picked_0[:, (2 * h + 1) * HALF : (2 * h + 2) * HALF], 1, h * HALF, (h + 1) * HALF)
+        for h in range(2):
+            nc.vector.tensor_copy(
+                as_words(woven_0[:, 4 * h * HALF : 4 * (h + 1) * HALF]),
+                picked_0[:, 2 * h * HALF : 2 * (h + 1) * HALF].rearrange("p (u n) -> p n u", u=2),
+            )
+        nc.vector.quantize_mx(out=codes_0_first[:].bitcast(FP8X4), scales=scales_0[:, 0:HALF], in_=woven_0[:, 0 : 4 * HALF])
+
+        picked_1 = keep.tile([P, 2 * S], U32, name="picked_1")
+        woven_1 = [keep.tile([P, 4 * CHUNK], BF16, name="woven_1_%d" % c, align_bytes=64) for c in range(CHUNKS)]
+        codes_1 = [keep.tile([P, CHUNK], U32, name="codes_1_%d" % c, align_bytes=64) for c in range(CHUNKS)]
+        scales_1 = [keep.tile([P, CHUNK], U8, name="scales_1_%d" % c, align_bytes=64) for c in range(CHUNKS)]
+        y_ps = [psum.tile([P, CHUNK], F32, name="y_ps_%d" % c) for c in range(CHUNKS)]
         moved = keep.tile([P, S], F32, name="moved")
-        cast(2)
-        nc.vector.tensor_copy(halves[:].rearrange("p (c u n) -> p c u n", u=2, n=CH)[:, :, 0, :], pairs[2].bitcast(U32).indirect(offs_sb[:]))
-        cast(3)
-        for c in range(NCH):
-            nc.vector.tensor_copy(halves[:, (2 * c + 1) * CH : (2 * c + 2) * CH], pairs[3].bitcast(U32).indirect(offs_sb[:, c * LC : (c + 1) * LC]))
-        for c in range(NCH):
-            cols = slice(c * CH, (c + 1) * CH)
-            nc.tensor.matmul_mx(out=y_ps[c][:], lhsT=w_words[:, 0, :].bitcast(FP8X4), lhsT_scale=w_scales[:, 0, :],
-                                rhs=codes0[:, cols].bitcast(FP8X4), rhs_scale=scales0[:, cols], start=True, stop=False)
-        for c in range(NCH):
-            nc.scalar.copy(quad1[c][:].bitcast(U32).rearrange("p (n u) -> p n u", u=2), halves[:, 2 * c * CH : (2 * c + 2) * CH].rearrange("p (u n) -> p n u", u=2))
-            nc.vector.quantize_mx(out=codes1[c][:].bitcast(FP8X4), scales=scales1[c][:], in_=quad1[c][:])
-            nc.tensor.matmul_mx(out=y_ps[c][:], lhsT=w_words[:, 1, :].bitcast(FP8X4), lhsT_scale=w_scales[:, 1, :],
-                                rhs=codes1[c][:].bitcast(FP8X4), rhs_scale=scales1[c][:], start=False, stop=True)
+        round_pair(2)
+        gather_pair(picked_1[:].rearrange("p (c u n) -> p c u n", u=2, n=CHUNK)[:, :, 0, :], 2, 0, S)
+        round_pair(3)
+
+        codes_0_second = keep.tile([P, HALF], U32, name="codes_0_second", tag="raw_0_0", align_bytes=64)
+        nc.vector.quantize_mx(out=codes_0_second[:].bitcast(FP8X4), scales=scales_0[:, HALF:S], in_=woven_0[:, 4 * HALF : 4 * S])
+        codes_0 = [half[:, first : first + CHUNK] for half in (codes_0_first, codes_0_second) for first in range(0, HALF, CHUNK)]
+
+        for c in range(CHUNKS):
+            gather_pair(picked_1[:, (2 * c + 1) * CHUNK : (2 * c + 2) * CHUNK], 3, c * CHUNK, (c + 1) * CHUNK)
+
+        def multiply(c, z, codes, scales):
+            nc.tensor.matmul_mx(
+                out=y_ps[c][:],
+                lhsT=w_words[:, z, :].bitcast(FP8X4),
+                lhsT_scale=w_scales[:, z, :],
+                rhs=codes.bitcast(FP8X4),
+                rhs_scale=scales,
+                start=(z == 0),
+                stop=(z == 1),
+            )
+
+        for c in range(CHUNKS):
+            multiply(c, 0, codes_0[c], scales_0[:, c * CHUNK : (c + 1) * CHUNK])
+        for c in range(CHUNKS):
+            nc.scalar.copy(
+                as_words(woven_1[c][:]),
+                picked_1[:, 2 * c * CHUNK : (2 * c + 2) * CHUNK].rearrange("p (u n) -> p n u", u=2),
+            )
+            nc.vector.quantize_mx(out=codes_1[c][:].bitcast(FP8X4), scales=scales_1[c][:], in_=woven_1[c][:])
+            multiply(c, 1, codes_1[c][:], scales_1[c][:])
 
         def weigh(c):
-            cols = slice(c * CH, (c + 1) * CH)
+            cols = slice(c * CHUNK, (c + 1) * CHUNK)
             nc.vector.tensor_tensor(moved[:, cols], y_ps[c][:], new_sb[:, cols], MULT)
 
-        def put(c0, c1):
-            cols = slice(c0 * CH, c1 * CH)
-            nc.vector.tensor_tensor(mem_sb[:].indirect(slot_sb[:, c0 * LC : c1 * LC]), moved[:, cols], kept[:, cols], ADD)
+        def scatter(first, last):
+            nc.vector.tensor_tensor(mem_sb[:].indirect(entries(slot_sb, first, last)), moved[:, first:last], kept[:, first:last], ADD)
 
         weigh(0)
         weigh(1)
-        put(0, 1)
-        weigh(2)
-        weigh(3)
-        put(1, NCH)
+        scatter(0, CHUNK)
+        for c in range(2, CHUNKS):
+            weigh(c)
+        scatter(CHUNK, S)
         nc.sync.dma_start(out=out, in_=mem_sb[:])

from contextlib import ExitStack

import concourse.mybir as mybir
from concourse.masks import make_identity

K, T, S, N, U = 1024, 1024, 512, 128, 1024
FLOPS = 2 * K * N * S

F32 = mybir.dt.float32
BF16 = mybir.dt.bfloat16
I32 = mybir.dt.int32
U32 = mybir.dt.uint32
U16 = mybir.dt.uint16
U8 = mybir.dt.uint8
FP8X4 = mybir.dt.float8_e4m3fn_x4
MULT = mybir.AluOpType.mult
ADD = mybir.AluOpType.add

P = 128
PER_COLUMN = 16
HALF = S // 2
CHUNK = 128
CHUNKS = S // CHUNK

PIECES = (
    ((0, 1024, 384),),
    ((0, 1024, 512),),
    ((0, 512, 512), (512, 512, 512)),
    ((0, 512, 512), (512, 512, 288)),
)


def tile_picked_ema_none_e_kernel(tc, xT, mem, w1_words, w1_scales, old, new, offs, slot, out):
    nc = tc.nc
    with ExitStack() as ctx:
        keep = ctx.enter_context(tc.tile_pool(name="keep", bufs=1))
        psum = ctx.enter_context(tc.psum_pool(name="psum", bufs=1))

        def entries(list_sb, first, last):
            return list_sb[:, first // PER_COLUMN : last // PER_COLUMN]

        offs_sb = keep.tile([P, S // PER_COLUMN], U16, name="offs_sb")
        slot_sb = keep.tile([P, S // PER_COLUMN], U16, name="slot_sb")
        mem_sb = keep.tile([P, U], F32, name="mem_sb")
        old_col = keep.tile([P, 4], F32, name="old_col")
        new_sb = keep.tile([P, S], F32, name="new_sb")
        w_words = keep.tile([P, 2, N], U32, name="w_words", align_bytes=64)
        w_scales = keep.tile([P, 2, N], U8, name="w_scales", align_bytes=64)
        ident = keep.tile([P, P], F32, name="ident")

        raw = {}
        for pair in range(4):
            for first, width, by_scalar in PIECES[pair]:
                label = "raw_%d_%d" % (pair, first)
                raw[pair, first] = keep.tile([P, 2, width], F32, name=label, tag=label, align_bytes=64)

        x_rows = xT.rearrange("(z p u e) t -> z u p e t", z=2, p=P, u=2, e=2)

        def load_x(pair, piece):
            first, width, by_scalar = PIECES[pair][piece]
            nc.sync.dma_start(out=raw[pair, first][:], in_=x_rows[pair // 2, pair % 2, :, :, first : first + width])

        make_identity(nc, ident[:])
        nc.sync.dma_start(out=old_col[:], in_=old[0, :].rearrange("(p c) -> p c", c=4))
        nc.sync.dma_start(out=mem_sb[:], in_=mem)
        nc.sync.dma_start(slot_sb[:], slot)
        load_x(0, 0)
        nc.sync.dma_start(offs_sb[:], offs)
        load_x(1, 0)
        load_x(2, 0)
        nc.gpsimd.memset(w_scales[:], 0)
        scale_rows = w1_scales.rearrange("z (q r) c -> r q z c", r=4)
        for r in range(4):
            nc.sync.dma_start(out=w_scales[r:P:32, :, :].bitcast(I32), in_=scale_rows[r].bitcast(I32))
        load_x(2, 1)
        load_x(3, 0)
        load_x(3, 1)
        nc.sync.dma_start(out=w_words[:].bitcast(I32), in_=w1_words.rearrange("z p n r -> p z (n r)").bitcast(I32))
        nc.sync.dma_start(out=new_sb[:], in_=new)

        old_ps = psum.tile([P, 4, P], F32, name="old_ps")
        for c in range(4):
            nc.tensor.transpose(old_ps[:, c, :], old_col[:, c : c + 1].to_broadcast([P, P]), ident[:])
        old_sb = keep.tile([P, S], F32, name="old_sb")
        nc.scalar.copy(old_sb[:].rearrange("p (n c) -> p n c", c=4), old_ps[:].rearrange("p c n -> p n c"))

        picked_mem = keep.tile([P, S], F32, name="picked_mem", tag="picked_mem", align_bytes=64)
        kept = keep.tile([P, S], F32, name="kept")
        nc.vector.tensor_copy(picked_mem[:], mem_sb[:].indirect(slot_sb[:]))
        nc.vector.tensor_tensor(kept[:], picked_mem[:], old_sb[:], MULT)

        window_0 = keep.tile([P, 2 * T], BF16, name="window_0", tag="picked_mem", align_bytes=64)
        windows_1_2 = keep.tile([P, 4 * T], BF16, name="windows_1_2", tag="raw_0_0", align_bytes=64)
        window_3 = keep.tile([P, 2 * T], BF16, name="window_3", tag="raw_2_0", align_bytes=64)
        windows = [window_0[:], windows_1_2[:, 0 : 2 * T], windows_1_2[:, 2 * T : 4 * T], window_3[:]]

        def round_pair(pair):
            dst = windows[pair].rearrange("p (t e) -> p t e", e=2)
            for first, width, by_scalar in PIECES[pair]:
                src = raw[pair, first][:].rearrange("p e t -> p t e")
                nc.scalar.copy(dst[:, first : first + by_scalar, :], src[:, 0:by_scalar, :])
                if by_scalar < width:
                    nc.vector.tensor_copy(dst[:, first + by_scalar : first + width, :], src[:, by_scalar:width, :])

        def gather_pair(dst, pair, first, last):
            nc.vector.tensor_copy(dst, windows[pair].bitcast(U32).indirect(entries(offs_sb, first, last)))

        def as_words(woven):
            return woven.bitcast(U32).rearrange("p (n u) -> p n u", u=2)

        picked_0 = keep.tile([P, 2 * S], U32, name="picked_0")
        woven_0 = keep.tile([P, 4 * S], BF16, name="woven_0", align_bytes=64)
        codes_0_first = keep.tile([P, HALF], U32, name="codes_0_first", align_bytes=64)
        scales_0 = keep.tile([P, S], U8, name="scales_0", align_bytes=64)
        round_pair(0)
        gather_pair(picked_0[:].rearrange("p (h u n) -> p h u n", u=2, n=HALF)[:, :, 0, :], 0, 0, S)
        round_pair(1)
        for h in range(2):
            gather_pair(picked_0[:, (2 * h + 1) * HALF : (2 * h + 2) * HALF], 1, h * HALF, (h + 1) * HALF)
        for h in range(2):
            nc.vector.tensor_copy(
                as_words(woven_0[:, 4 * h * HALF : 4 * (h + 1) * HALF]),
                picked_0[:, 2 * h * HALF : 2 * (h + 1) * HALF].rearrange("p (u n) -> p n u", u=2),
            )
        nc.vector.quantize_mx(out=codes_0_first[:].bitcast(FP8X4), scales=scales_0[:, 0:HALF], in_=woven_0[:, 0 : 4 * HALF])

        picked_1 = keep.tile([P, 2 * S], U32, name="picked_1")
        woven_1 = [keep.tile([P, 4 * CHUNK], BF16, name="woven_1_%d" % c, align_bytes=64) for c in range(CHUNKS)]
        codes_1 = [keep.tile([P, CHUNK], U32, name="codes_1_%d" % c, align_bytes=64) for c in range(CHUNKS)]
        scales_1 = [keep.tile([P, CHUNK], U8, name="scales_1_%d" % c, align_bytes=64) for c in range(CHUNKS)]
        y_ps = [psum.tile([P, CHUNK], F32, name="y_ps_%d" % c) for c in range(CHUNKS)]
        moved = keep.tile([P, S], F32, name="moved")
        round_pair(2)
        gather_pair(picked_1[:].rearrange("p (c u n) -> p c u n", u=2, n=CHUNK)[:, :, 0, :], 2, 0, S)
        round_pair(3)

        codes_0_second = keep.tile([P, HALF], U32, name="codes_0_second", tag="raw_0_0", align_bytes=64)
        nc.vector.quantize_mx(out=codes_0_second[:].bitcast(FP8X4), scales=scales_0[:, HALF:S], in_=woven_0[:, 4 * HALF : 4 * S])
        codes_0 = [half[:, first : first + CHUNK] for half in (codes_0_first, codes_0_second) for first in range(0, HALF, CHUNK)]

        for c in range(CHUNKS):
            gather_pair(picked_1[:, (2 * c + 1) * CHUNK : (2 * c + 2) * CHUNK], 3, c * CHUNK, (c + 1) * CHUNK)

        def multiply(c, z, codes, scales):
            nc.tensor.matmul_mx(
                out=y_ps[c][:],
                lhsT=w_words[:, z, :].bitcast(FP8X4),
                lhsT_scale=w_scales[:, z, :],
                rhs=codes.bitcast(FP8X4),
                rhs_scale=scales,
                start=(z == 0),
                stop=(z == 1),
            )

        for c in range(CHUNKS):
            multiply(c, 0, codes_0[c], scales_0[:, c * CHUNK : (c + 1) * CHUNK])
        for c in range(CHUNKS):
            nc.scalar.copy(
                as_words(woven_1[c][:]),
                picked_1[:, 2 * c * CHUNK : (2 * c + 2) * CHUNK].rearrange("p (u n) -> p n u", u=2),
            )
            nc.vector.quantize_mx(out=codes_1[c][:].bitcast(FP8X4), scales=scales_1[c][:], in_=woven_1[c][:])
            multiply(c, 1, codes_1[c][:], scales_1[c][:])

        def weigh(c):
            cols = slice(c * CHUNK, (c + 1) * CHUNK)
            nc.vector.tensor_tensor(moved[:, cols], y_ps[c][:], new_sb[:, cols], MULT)

        def scatter(first, last):
            nc.vector.tensor_tensor(mem_sb[:].indirect(entries(slot_sb, first, last)), moved[:, first:last], kept[:, first:last], ADD)

        weigh(0)
        weigh(1)
        scatter(0, CHUNK)
        for c in range(2, CHUNKS):
            weigh(c)
        scatter(CHUNK, S)
        nc.sync.dma_start(out=out, in_=mem_sb[:])
